import numpy as np
import ml_dtypes


def mxq(x, axis, fmt="e4m3"):
    dtype, down = {"e4m3": (ml_dtypes.float8_e4m3fn, 7), "e5m2": (ml_dtypes.float8_e5m2, 14)}[fmt]
    v = np.moveaxis(np.asarray(x, np.float32).astype(ml_dtypes.bfloat16).astype(np.float64), axis, -1)
    blocks = v.reshape(v.shape[:-1] + (-1, 32))
    amax = np.abs(blocks).max(-1, keepdims=True)
    byte = np.maximum(np.where(amax > 0, np.frexp(amax)[1] - 1 + 127, 0) - down, 1)
    scale = np.exp2(byte - 127.0)
    codes = (blocks / scale).astype(np.float32).astype(dtype).astype(np.float64)
    return np.moveaxis((codes * scale).reshape(v.shape), -1, axis)


WIDE = False


def mx_kscale(k):
    if not WIDE:
        return np.ones(k)
    levels = np.array([10, -10, 5, -5, 0])
    if k % 512:
        return np.exp2(np.random.permutation(np.resize(levels, k // 32))).repeat(32)
    a = np.empty((k // 512, 16))
    for p in range(k // 512):
        a[p, :8] = np.random.permutation(np.resize(levels, 8))
        for g in range(8):
            far = levels[np.abs(levels - a[p, g]) >= 10]
            a[p, g + 8] = far[np.random.randint(len(far))]
    return np.exp2(a.ravel()).repeat(32)


def f64(x):
    return np.asarray(x).astype(np.float64)


def striped(idx):
    return np.tile(idx.reshape(-1, 16).T, (8, 1)).astype(np.uint16)


def unstriped(offs):
    return offs[:16].T.reshape(-1).astype(np.int64)


def striped8(idx):
    return np.concatenate([x.reshape(-1, 16).T for x in idx]).astype(np.uint16)


def runs(offs, k):
    lists = np.stack([offs[16 * r : 16 * r + 16].T.reshape(-1) for r in range(8)]).astype(np.int64)
    return lists[np.arange(k) % 512 // 64]


def pack_weight(w):
    k, n = w.shape
    w = f64(np.asarray(w, np.float32).astype(ml_dtypes.bfloat16)).reshape(k // 32, 32, n)
    amax = np.abs(w).max(1)
    byte = np.clip(np.where(amax > 0, np.frexp(amax)[1] - 1 + 127 - 7, 1), 1, 254)
    scaled = (w * np.exp2(127.0 - byte)[:, None, :]).reshape(k, n).astype(np.float32)
    words = np.ascontiguousarray(scaled.reshape(k // 512, 128, 4, n).transpose(0, 1, 3, 2)).astype(ml_dtypes.float8_e4m3fn).view(np.uint8)
    return words, np.ascontiguousarray(byte.astype(np.uint8).reshape(k // 512, 16, n))


def unpack_weight(words, scales):
    g, p, n, _ = words.shape
    vals = np.ascontiguousarray(words).view(ml_dtypes.float8_e4m3fn).astype(np.float64) * np.repeat(np.exp2(scales.astype(np.float64) - 127.0), 8, axis=1)[..., None]
    return vals.transpose(0, 1, 3, 2).reshape(g * 512, n)


E2M1 = np.array([0.0, 0.5, 1.0, 1.5, 2.0, 3.0, 4.0, 6.0, -0.0, -0.5, -1.0, -1.5, -2.0, -3.0, -4.0, -6.0])


def pack_fp4(w):
    k, n = w.shape
    w = f64(np.asarray(w, np.float32).astype(ml_dtypes.bfloat16)).reshape(k // 32, 32, n)
    amax = np.abs(w).max(1)
    mant, ex = np.frexp(amax / 6.0)
    byte = np.clip(np.where(amax > 0, np.where(mant > 0.5, ex, ex - 1) + 127, 1), 1, 254)
    scaled = (w * np.exp2(127.0 - byte)[:, None, :]).reshape(k, n).astype(np.float32)
    c = np.ascontiguousarray(scaled.reshape(k // 512, 128, 4, n).transpose(0, 1, 3, 2)).astype(ml_dtypes.float4_e2m1fn).view(np.uint8) & 0xF
    words = (c[..., 0::2] | (c[..., 1::2] << 4)).reshape(k // 512, 128, 2 * n)
    return np.ascontiguousarray(words), np.ascontiguousarray(byte.astype(np.uint8).reshape(k // 512, 16, n))


def unpack_fp4(words, scales):
    g, _, n = scales.shape
    words = np.ascontiguousarray(words).reshape(g, 128, n, 2)
    nib = np.empty((g, 128, n, 4), np.uint8)
    nib[..., 0::2] = words & 0xF
    nib[..., 1::2] = words >> 4
    vals = E2M1[nib] * np.repeat(np.exp2(scales.astype(np.float64) - 127.0), 8, axis=1)[..., None]
    return vals.transpose(0, 1, 3, 2).reshape(g * 512, n)


def sigmoid(v):
    return 1.0 / (1.0 + np.exp(-np.maximum(v, -700.0)))

def planes(y):
    n, m = y.shape
    v = y.astype(np.float32).astype(ml_dtypes.bfloat16).astype(np.float64).reshape(n // 32, 32, m)
    top = np.abs(v).max(1)
    byte = np.clip(np.where(top > 0, np.frexp(top)[1] - 1 + 127 - 7, 1), 1, 254)
    codes = (v * np.exp2(127.0 - byte)[:, None, :]).reshape(n, m).astype(np.float32).astype(ml_dtypes.float8_e4m3fn).view(np.uint8)
    words = codes.reshape(n // 512, 128, 4, m).transpose(0, 1, 3, 2)
    return np.ascontiguousarray(words), np.ascontiguousarray(byte.astype(np.uint8).reshape(n // 512, 16, m))


K, T, S, N, H, W = 512, 2048, 512, 512, 512, 2048


def setup_inputs():
    n = np.random.standard_normal
    s = mx_kscale(K)[:, None]
    u = mx_kscale(H)
    packed_xT = pack_weight(n((K, T)) * s)
    packed_w1 = pack_fp4(n((K, H)) / np.sqrt(K) / s)
    packed_w2 = pack_fp4(n((K, H)) / np.sqrt(K) / s)
    packed_w3 = pack_fp4(n((H, N)) / np.sqrt(H) / u[:, None])
    return {
        "x_words": packed_xT[0],
        "x_scales": packed_xT[1],
        "w1_words": packed_w1[0],
        "w1_scales": packed_w1[1],
        "w2_words": packed_w2[0],
        "w2_scales": packed_w2[1],
        "gn": (np.random.uniform(0.5, 1.5, (H, 1)) * u[:, None]).astype(np.float32),
        "w3_words": packed_w3[0],
        "w3_scales": packed_w3[1],
        "sl": np.random.uniform(1.5, 3.0, (N, 1)).astype(np.float32),
        "th": (0.5 * n((N, 1))).astype(np.float32),
        "offs": striped(np.random.permutation(T)[:S]),
        "two": striped(np.random.permutation(T)[:S]),
        "n1": striped8(np.stack([np.random.permutation(S) for _ in range(8)])),
        "n2": striped8(np.stack([np.random.permutation(S) for _ in range(8)])),
        "n3": striped(np.random.randint(0, S, W)),
    }


def reference(x_words, x_scales, w1_words, w1_scales, w2_words, w2_scales, gn, w3_words, w3_scales, sl, th, offs, two, n1, n2, n3):
    xq = unpack_weight(x_words, x_scales)[:, unstriped(offs)]
    y = unpack_fp4(w1_words, w1_scales).T @ xq
    x_two = unpack_weight(x_words, x_scales)[:, unstriped(two)]
    d = unpack_fp4(w2_words, w2_scales).T @ x_two
    z = f64(gn) * (y * (sigmoid(d[np.arange(H)[:, None], runs(n2, H)])) - (0.5 * (y[np.arange(H)[:, None], runs(n1, H)])))
    h = unpack_fp4(w3_words, w3_scales).T @ mxq(z, 0, "e4m3")
    sg = sigmoid(f64(sl) * (h[:, unstriped(n3)] - f64(th)))
    cnt = sg.reshape(N, S, 4).sum(axis=2)
    out_0 = np.maximum(h, cnt + -1.5)
    return (out_0,) + planes(out_0)

@@ -1,0 +1,207 @@
+from contextlib import ExitStack
+
+import concourse.mybir as mybir
+
+K, T, S, N, H, W = 512, 2048, 512, 512, 512, 2048
+FLOPS = 3 * 2 * 512 * 512 * 512
+
+F32 = mybir.dt.float32
+BF16 = mybir.dt.bfloat16
+I32 = mybir.dt.int32
+U32 = mybir.dt.uint32
+U16 = mybir.dt.uint16
+U8 = mybir.dt.uint8
+FP8X4 = mybir.dt.float8_e4m3fn_x4
+FP4X4 = mybir.dt.float4_e2m1fn_x4
+ACT = mybir.ActivationFunctionType
+ALU = mybir.AluOpType
+AXIS = mybir.AxisListType
+
+P = 128
+PACK = 4
+MEMBERS = 4
+Z_CHUNKS = ((0, 256), (256, 512))
+OUT_CHUNKS = ((0, 128), (128, 256), (256, 384), (384, 448), (448, 512))
+H_WINDOW = 1024
+
+
+def load_scale_rows(queue, tile, scales):
+    for q in range(4):
+        queue.dma_start(
+            out=tile[32 * q : 32 * q + 4, :].bitcast(I32),
+            in_=scales[0, 4 * q : 4 * q + 4, :].bitcast(I32),
+        )
+
+
+def tile_picked_twlgatebegc_none_po_kernel(
+    tc, x_words, x_scales, w1_words, w1_scales, w2_words, w2_scales, gn, w3_words, w3_scales,
+    sl, th, offs, two, n1, n2, n3, out_0, out_1, out_2,
+):
+    nc = tc.nc
+    with ExitStack() as ctx:
+        keep = ctx.enter_context(tc.tile_pool(name="keep", bufs=1))
+        ring = ctx.enter_context(tc.tile_pool(name="ring", bufs=4))
+        psum = ctx.enter_context(tc.psum_pool(name="psum", bufs=1))
+
+        def new(name, shape, dtype):
+            return keep.tile(shape, dtype, name=name, align_bytes=64)
+
+        offs_t = new("offs_t", [P, S // 16], U16)
+        two_t = new("two_t", [P, S // 16], U16)
+        n1_t = new("n1_t", [P, S // 16], U16)
+        n2_t = new("n2_t", [P, S // 16], U16)
+        n3_t = new("n3_t", [P, W // 16], U16)
+        xw = new("xw", [P, T], U32)
+        xs = new("xs", [P, T], U8)
+        raw_w = [new(f"raw_w{i}", [P, 2 * H], U8) for i in range(3)]
+        raw_s = [new(f"raw_s{i}", [P, H], U8) for i in range(3)]
+        w = [new(f"w{i}", [P, 2 * H], U8) for i in range(3)]
+        ws = [new(f"ws{i}", [P, H], U8) for i in range(2)]
+        gn_t = new("gn_t", [P, PACK], F32)
+        sl_t = new("sl_t", [P, PACK], F32)
+        th_t = new("th_t", [P, PACK], F32)
+        slth = new("slth", [P, PACK], F32)
+        bias = new("bias", [P, PACK], F32)
+        h = [new(f"h{t}", [P, H_WINDOW], F32) for t in range(PACK)]
+
+        nc.vector.memset(xs[:].bitcast(I32), 0)
+        nc.vector.memset(raw_s[1][:].bitcast(I32), 0)
+        nc.vector.memset(raw_s[0][:].bitcast(I32), 0)
+        nc.vector.memset(raw_s[2][:].bitcast(I32), 0)
+
+        nc.sync.dma_start(two_t[:], two)
+        nc.sync.dma_start(out=xw[:].bitcast(I32), in_=x_words[0].rearrange("p n t -> p (n t)").bitcast(I32))
+        load_scale_rows(nc.scalar, xs, x_scales)
+        load_scale_rows(nc.scalar, raw_s[1], w2_scales)
+        nc.sync.dma_start(out=raw_w[1][:].bitcast(I32), in_=w2_words[0].bitcast(I32))
+        nc.sync.dma_start(offs_t[:], offs)
+        nc.sync.dma_start(out=raw_w[0][:].bitcast(I32), in_=w1_words[0].bitcast(I32))
+        nc.sync.dma_start(out=raw_w[2][:].bitcast(I32), in_=w3_words[0].bitcast(I32))
+        load_scale_rows(nc.sync, raw_s[0], w1_scales)
+        nc.sync.dma_start(n2_t[:], n2)
+        nc.sync.dma_start(out=gn_t[:], in_=gn.rearrange("(p t) o -> p (t o)", t=PACK))
+        nc.sync.dma_start(n1_t[:], n1)
+        nc.sync.dma_start(n3_t[:], n3)
+        load_scale_rows(nc.sync, raw_s[2], w3_scales)
+        nc.sync.dma_start(out=sl_t[:], in_=sl.rearrange("(p t) o -> p (t o)", t=PACK))
+        nc.sync.dma_start(out=th_t[:], in_=th.rearrange("(p t) o -> p (t o)", t=PACK))
+        for t in range(PACK):
+            nc.vector.memset(h[t][:, S:], 0.0)
+
+        def deal_words(i):
+            nc.scalar.copy(
+                out=w[i][:].bitcast(U16).rearrange("p (t m) -> p t m", t=PACK),
+                in_=raw_w[i][:].bitcast(U16).rearrange("p (m t) -> p t m", t=PACK),
+            )
+
+        def deal_scales(i):
+            nc.vector.tensor_copy(
+                out=ws[i][:].rearrange("p (t m) -> p t m", t=PACK),
+                in_=raw_s[i][:].rearrange("p (m t) -> p t m", t=PACK),
+            )
+
+        def product(out, i, t, codes, scales):
+            nc.tensor.matmul_mx(
+                out=out,
+                lhsT=w[i][:, 2 * P * t : 2 * P * (t + 1)].bitcast(FP4X4),
+                lhsT_scale=ws[i][:, P * t : P * (t + 1)],
+                rhs=codes.bitcast(FP8X4),
+                rhs_scale=scales,
+                start=True,
+                stop=True,
+            )
+
+        def bank(b, name):
+            return psum.tile([P, S], F32, name=name, tag=f"bank{b}")
+
+        xd_s = new("xd_s", [P, S], U8)
+        xd_w = new("xd_w", [P, S], U32)
+        xy_s = new("xy_s", [P, S], U8)
+        xy_w = new("xy_w", [P, S], U32)
+        deal_words(1)
+        deal_words(0)
+        deal_words(2)
+        nc.vector.tensor_copy(xd_s[:], xs[:].indirect(two_t[:]))
+        deal_scales(1)
+        nc.vector.tensor_copy(xd_w[:], xw[:].indirect(two_t[:]))
+        nc.vector.tensor_copy(xy_s[:], xs[:].indirect(offs_t[:]))
+        deal_scales(0)
+        nc.vector.tensor_copy(xy_w[:], xw[:].indirect(offs_t[:]))
+        nc.gpsimd.tensor_tensor(slth[:], sl_t[:], th_t[:], ALU.mult)
+        nc.gpsimd.tensor_scalar(bias[:], slth[:], -1.0, 0.0, ALU.mult, ALU.add)
+
+        gate = [new(f"gate{t}", [P, S], F32) for t in range(PACK)]
+        gy = [new(f"gy{t}", [P, S], F32) for t in range(PACK)]
+        for t in range(PACK):
+            d_ps = bank(t, f"d{t}")
+            product(d_ps[:], 1, t, xd_w[:], xd_s[:])
+            nc.scalar.activation(gate[t][:], d_ps[:], ACT.Sigmoid)
+        ws.append(new("ws1", [P, H], U8))
+        deal_scales(2)
+        for t in range(PACK):
+            y_ps = bank(PACK + t, f"y{t}")
+            product(y_ps[:], 0, t, xy_w[:], xy_s[:])
+            nc.scalar.activation(gy[t][:], y_ps[:], ACT.Copy, scale=gn_t[:, t : t + 1])
+
+        for c, (c0, c1) in enumerate(Z_CHUNKS):
+            n = c1 - c0
+            gated = new(f"gated{c}", [P, PACK, n], F32)
+            half = new(f"half{c}", [P, PACK, n], F32)
+            zb = new(f"zb{c}", [P, n * PACK], BF16)
+            zw = new(f"zw{c}", [P, n], U32)
+            zs = new(f"zs{c}", [P, n], U8)
+            for t in range(PACK):
+                nc.vector.tensor_tensor(
+                    gated[:, t, :], gate[t][:].indirect(n2_t[:, c0 // 16 : c1 // 16]), gy[t][:, c0:c1], ALU.mult
+                )
+                nc.scalar.activation(
+                    half[:, t, :], gy[t][:].indirect(n1_t[:, c0 // 16 : c1 // 16]), ACT.Copy, scale=0.5
+                )
+            nc.vector.tensor_tensor(
+                zb[:].rearrange("p (c i t) -> p c t i", i=4, t=PACK),
+                gated[:].rearrange("p t (c i) -> p c t i", i=4),
+                half[:].rearrange("p t (c i) -> p c t i", i=4),
+                ALU.subtract,
+            )
+            nc.vector.quantize_mx(out=zw[:].bitcast(FP8X4), scales=zs[:], in_=zb[:])
+            for t in range(PACK):
+                h_ps = bank(PACK * c + t, f"h{c}_{t}")
+                product(h_ps[:, :n], 2, t, zw[:], zs[:])
+                if t == 0:
+                    nc.scalar.copy(h[t][:, c0:c1], h_ps[:, :n])
+                else:
+                    nc.vector.tensor_copy(h[t][:, c0:c1], h_ps[:, :n])
+
+        out_rows = out_0.rearrange("(p t) c -> p t c", t=PACK)
+        out_words = out_1[0].rearrange("p n t -> p (n t)").bitcast(I32)
+        osc = new("osc", [P, S], U8)
+        for c, (c0, c1) in enumerate(OUT_CHUNKS):
+            n = c1 - c0
+            res = new(f"res{c}", [P, PACK, n], F32)
+            rb = new(f"rb{c}", [P, n * PACK], BF16)
+            ow = new(f"ow{c}", [P, n], U32)
+            for t in range(PACK):
+                sg = ring.tile([P, MEMBERS * n], F32, name="sg")
+                cnt = ring.tile([P, n], F32, name="cnt")
+                nc.scalar.activation(
+                    sg[:],
+                    h[t][:].indirect(n3_t[:, MEMBERS * c0 // 16 : MEMBERS * c1 // 16]),
+                    ACT.Sigmoid,
+                    bias=bias[:, t : t + 1],
+                    scale=sl_t[:, t : t + 1],
+                )
+                nc.vector.tensor_reduce(cnt[:], sg[:].rearrange("p (c m) -> p c m", m=MEMBERS), AXIS.X, ALU.add)
+                nc.vector.scalar_tensor_tensor(res[:, t, :], cnt[:], -1.5, h[t][:, c0:c1], ALU.add, ALU.max)
+            nc.sync.dma_start(out=out_rows[:, :, c0:c1], in_=res[:])
+            nc.vector.tensor_copy(
+                rb[:].rearrange("p (c i t) -> p c t i", i=4, t=PACK),
+                res[:].rearrange("p t (c i) -> p c t i", i=4),
+            )
+            nc.vector.quantize_mx(out=ow[:].bitcast(FP8X4), scales=osc[:, c0:c1], in_=rb[:])
+            nc.sync.dma_start(out=out_words[:, c0:c1], in_=ow[:].bitcast(I32))
+        for q in range(4):
+            queue = nc.scalar if q % 2 == 0 else nc.sync
+            queue.dma_start(
+                out=out_2[0, 4 * q : 4 * q + 4, :].bitcast(I32),
+                in_=osc[32 * q : 32 * q + 4, :].bitcast(I32),
+            )

@@ -20,14 +20,14 @@ AXIS = mybir.AxisListType
 P = 128
 PACK = 4
 MEMBERS = 4
-Z_CHUNKS = ((0, 256), (256, 512))
+Z_CHUNKS = ((0, 256), (256, 384), (384, 512))
 OUT_CHUNKS = ((0, 128), (128, 256), (256, 384), (384, 448), (448, 512))
 H_WINDOW = 1024
 
 
-def load_scale_rows(queue, tile, scales):
+def load_scale_rows(queues, tile, scales):
     for q in range(4):
-        queue.dma_start(
+        queues[q].dma_start(
             out=tile[32 * q : 32 * q + 4, :].bitcast(I32),
             in_=scales[0, 4 * q : 4 * q + 4, :].bitcast(I32),
         )
@@ -43,8 +43,8 @@ def tile_picked_twlgatebegc_none_po_kernel(
         ring = ctx.enter_context(tc.tile_pool(name="ring", bufs=4))
         psum = ctx.enter_context(tc.psum_pool(name="psum", bufs=1))
 
-        def new(name, shape, dtype):
-            return keep.tile(shape, dtype, name=name, align_bytes=64)
+        def new(name, shape, dtype, tag=""):
+            return keep.tile(shape, dtype, name=name, align_bytes=64, tag=tag or name)
 
         offs_t = new("offs_t", [P, S // 16], U16)
         two_t = new("two_t", [P, S // 16], U16)
@@ -56,7 +56,7 @@ def tile_picked_twlgatebegc_none_po_kernel(
         raw_w = [new(f"raw_w{i}", [P, 2 * H], U8) for i in range(3)]
         raw_s = [new(f"raw_s{i}", [P, H], U8) for i in range(3)]
         w = [new(f"w{i}", [P, 2 * H], U8) for i in range(3)]
-        ws = [new(f"ws{i}", [P, H], U8) for i in range(2)]
+        ws = {}
         gn_t = new("gn_t", [P, PACK], F32)
         sl_t = new("sl_t", [P, PACK], F32)
         th_t = new("th_t", [P, PACK], F32)
@@ -64,25 +64,25 @@ def tile_picked_twlgatebegc_none_po_kernel(
         bias = new("bias", [P, PACK], F32)
         h = [new(f"h{t}", [P, H_WINDOW], F32) for t in range(PACK)]
 
-        nc.vector.memset(xs[:].bitcast(I32), 0)
+        nc.gpsimd.memset(xs[:].bitcast(I32), 0)
+        nc.gpsimd.memset(raw_s[0][:].bitcast(I32), 0)
         nc.vector.memset(raw_s[1][:].bitcast(I32), 0)
-        nc.vector.memset(raw_s[0][:].bitcast(I32), 0)
         nc.vector.memset(raw_s[2][:].bitcast(I32), 0)
 
         nc.sync.dma_start(two_t[:], two)
-        nc.sync.dma_start(out=xw[:].bitcast(I32), in_=x_words[0].rearrange("p n t -> p (n t)").bitcast(I32))
-        load_scale_rows(nc.scalar, xs, x_scales)
-        load_scale_rows(nc.scalar, raw_s[1], w2_scales)
-        nc.sync.dma_start(out=raw_w[1][:].bitcast(I32), in_=w2_words[0].bitcast(I32))
         nc.sync.dma_start(offs_t[:], offs)
+        load_scale_rows([nc.scalar, nc.scalar, nc.sync, nc.sync], xs, x_scales)
+        nc.sync.dma_start(out=xw[:].bitcast(I32), in_=x_words[0].rearrange("p n t -> p (n t)").bitcast(I32))
+        load_scale_rows([nc.sync] * 4, raw_s[1], w2_scales)
+        load_scale_rows([nc.gpsimd] * 4, raw_s[0], w1_scales)
+        nc.sync.dma_start(out=raw_w[1][:].bitcast(I32), in_=w2_words[0].bitcast(I32))
         nc.sync.dma_start(out=raw_w[0][:].bitcast(I32), in_=w1_words[0].bitcast(I32))
-        nc.sync.dma_start(out=raw_w[2][:].bitcast(I32), in_=w3_words[0].bitcast(I32))
-        load_scale_rows(nc.sync, raw_s[0], w1_scales)
         nc.sync.dma_start(n2_t[:], n2)
         nc.sync.dma_start(out=gn_t[:], in_=gn.rearrange("(p t) o -> p (t o)", t=PACK))
         nc.sync.dma_start(n1_t[:], n1)
+        nc.sync.dma_start(out=raw_w[2][:].bitcast(I32), in_=w3_words[0].bitcast(I32))
+        load_scale_rows([nc.sync] * 4, raw_s[2], w3_scales)
         nc.sync.dma_start(n3_t[:], n3)
-        load_scale_rows(nc.sync, raw_s[2], w3_scales)
         nc.sync.dma_start(out=sl_t[:], in_=sl.rearrange("(p t) o -> p (t o)", t=PACK))
         nc.sync.dma_start(out=th_t[:], in_=th.rearrange("(p t) o -> p (t o)", t=PACK))
         for t in range(PACK):
@@ -94,8 +94,9 @@ def tile_picked_twlgatebegc_none_po_kernel(
                 in_=raw_w[i][:].bitcast(U16).rearrange("p (m t) -> p t m", t=PACK),
             )
 
-        def deal_scales(i):
-            nc.vector.tensor_copy(
+        def deal_scales(i, engine, tag):
+            ws[i] = new(f"ws{i}", [P, H], U8, tag)
+            engine.tensor_copy(
                 out=ws[i][:].rearrange("p (t m) -> p t m", t=PACK),
                 in_=raw_s[i][:].rearrange("p (m t) -> p t m", t=PACK),
             )
@@ -120,57 +121,79 @@ def tile_picked_twlgatebegc_none_po_kernel(
         xy_w = new("xy_w", [P, S], U32)
         deal_words(1)
         deal_words(0)
-        deal_words(2)
         nc.vector.tensor_copy(xd_s[:], xs[:].indirect(two_t[:]))
-        deal_scales(1)
         nc.vector.tensor_copy(xd_w[:], xw[:].indirect(two_t[:]))
         nc.vector.tensor_copy(xy_s[:], xs[:].indirect(offs_t[:]))
-        deal_scales(0)
-        nc.vector.tensor_copy(xy_w[:], xw[:].indirect(offs_t[:]))
+        halves = ((0, S // 2), (S // 2, S))
+        for c0, c1 in halves:
+            nc.vector.tensor_copy(xy_w[:, c0:c1], xw[:].indirect(offs_t[:, c0 // 16 : c1 // 16]))
+        deal_scales(1, nc.gpsimd, "ws1")
+        deal_scales(0, nc.gpsimd, "raw_s1")
+        nc.gpsimd.tensor_copy(
+            out=w[2][:].rearrange("p (t m b) -> p t m b", t=PACK, b=2),
+            in_=raw_w[2][:].rearrange("p (m t b) -> p t m b", t=PACK, b=2),
+        )
+        deal_scales(2, nc.gpsimd, "ws2")
         nc.gpsimd.tensor_tensor(slth[:], sl_t[:], th_t[:], ALU.mult)
         nc.gpsimd.tensor_scalar(bias[:], slth[:], -1.0, 0.0, ALU.mult, ALU.add)
 
-        gate = [new(f"gate{t}", [P, S], F32) for t in range(PACK)]
         gy = [new(f"gy{t}", [P, S], F32) for t in range(PACK)]
+        gated = new("gated", [P, PACK, S], F32)
         for t in range(PACK):
             d_ps = bank(t, f"d{t}")
             product(d_ps[:], 1, t, xd_w[:], xd_s[:])
-            nc.scalar.activation(gate[t][:], d_ps[:], ACT.Sigmoid)
-        ws.append(new("ws1", [P, H], U8))
-        deal_scales(2)
-        for t in range(PACK):
+            nc.scalar.activation(h[t][:, :S], d_ps[:], ACT.Sigmoid)
+        for b, (c0, c1) in zip((PACK, 0), halves):
+            y_ps = bank(b, f"y0_{c0}")
+            product(y_ps[:, c0:c1], 0, 0, xy_w[:, c0:c1], xy_s[:, c0:c1])
+            nc.vector.tensor_scalar(gy[0][:, c0:c1], y_ps[:, c0:c1], gn_t[:, 0:1], None, ALU.mult)
+        for t in range(1, PACK):
             y_ps = bank(PACK + t, f"y{t}")
             product(y_ps[:], 0, t, xy_w[:], xy_s[:])
             nc.scalar.activation(gy[t][:], y_ps[:], ACT.Copy, scale=gn_t[:, t : t + 1])
+        for t in range(PACK):
+            nc.vector.tensor_tensor(gated[:, t, :], h[t][:].indirect(n2_t[:]), gy[t][:], ALU.mult)
 
-        for c, (c0, c1) in enumerate(Z_CHUNKS):
-            n = c1 - c0
-            gated = new(f"gated{c}", [P, PACK, n], F32)
-            half = new(f"half{c}", [P, PACK, n], F32)
-            zb = new(f"zb{c}", [P, n * PACK], BF16)
-            zw = new(f"zw{c}", [P, n], U32)
-            zs = new(f"zs{c}", [P, n], U8)
+        zw = new("zw", [P, S], U32)
+        zs = new("zs", [P, S], U8)
+        zb = [new(f"zb{c}", [P, (c1 - c0) * PACK], BF16) for c, (c0, c1) in enumerate(Z_CHUNKS)]
+
+        def combine(c):
+            c0, c1 = Z_CHUNKS[c]
+            half = new(f"half{c}", [P, PACK, c1 - c0], F32)
             for t in range(PACK):
-                nc.vector.tensor_tensor(
-                    gated[:, t, :], gate[t][:].indirect(n2_t[:, c0 // 16 : c1 // 16]), gy[t][:, c0:c1], ALU.mult
-                )
                 nc.scalar.activation(
                     half[:, t, :], gy[t][:].indirect(n1_t[:, c0 // 16 : c1 // 16]), ACT.Copy, scale=0.5
                 )
             nc.vector.tensor_tensor(
-                zb[:].rearrange("p (c i t) -> p c t i", i=4, t=PACK),
-                gated[:].rearrange("p t (c i) -> p c t i", i=4),
+                zb[c][:].rearrange("p (c i t) -> p c t i", i=4, t=PACK),
+                gated[:, :, c0:c1].rearrange("p t (c i) -> p c t i", i=4),
                 half[:].rearrange("p t (c i) -> p c t i", i=4),
                 ALU.subtract,
             )
-            nc.vector.quantize_mx(out=zw[:].bitcast(FP8X4), scales=zs[:], in_=zb[:])
-            for t in range(PACK):
-                h_ps = bank(PACK * c + t, f"h{c}_{t}")
-                product(h_ps[:, :n], 2, t, zw[:], zs[:])
-                if t == 0:
-                    nc.scalar.copy(h[t][:, c0:c1], h_ps[:, :n])
-                else:
-                    nc.vector.tensor_copy(h[t][:, c0:c1], h_ps[:, :n])
+
+        def quantise(c):
+            c0, c1 = Z_CHUNKS[c]
+            nc.vector.quantize_mx(out=zw[:, c0:c1].bitcast(FP8X4), scales=zs[:, c0:c1], in_=zb[c][:])
+
+        combine(0)
+        for c in range(1, len(Z_CHUNKS)):
+            combine(c)
+            quantise(c - 1)
+        quantise(len(Z_CHUNKS) - 1)
+
+        early = bank(0, "h0_early")
+        for c0, c1 in Z_CHUNKS[:-1]:
+            product(early[:, c0:c1], 2, 0, zw[:, c0:c1], zs[:, c0:c1])
+        last0 = Z_CHUNKS[-1][0]
+        nc.scalar.copy(h[0][:, :last0], early[:, :last0])
+        late = bank(1, "h0_late")
+        product(late[:, last0:], 2, 0, zw[:, last0:], zs[:, last0:])
+        nc.scalar.copy(h[0][:, last0:S], late[:, last0:])
+        for t in range(1, PACK):
+            h_ps = bank(1 + t, f"h{t}_ps")
+            product(h_ps[:], 2, t, zw[:], zs[:])
+            nc.vector.tensor_copy(h[t][:, :S], h_ps[:])
 
         out_rows = out_0.rearrange("(p t) c -> p t c", t=PACK)
         out_words = out_1[0].rearrange("p n t -> p (n t)").bitcast(I32)

@@ -55,17 +55,16 @@ def tile_picked_twlgatebegc_none_po_kernel(
         xs = new("xs", [P, T], U8)
         raw_w = [new(f"raw_w{i}", [P, 2 * H], U8) for i in range(3)]
         raw_s = [new(f"raw_s{i}", [P, H], U8) for i in range(3)]
-        w = [new(f"w{i}", [P, 2 * H], U8) for i in range(3)]
+        w = [new(f"w{i}", [P, 2 * H], U8) for i in range(2)]
         ws = {}
         gn_t = new("gn_t", [P, PACK], F32)
         sl_t = new("sl_t", [P, PACK], F32)
         th_t = new("th_t", [P, PACK], F32)
-        slth = new("slth", [P, PACK], F32)
         bias = new("bias", [P, PACK], F32)
         h = [new(f"h{t}", [P, H_WINDOW], F32) for t in range(PACK)]
 
         nc.gpsimd.memset(xs[:].bitcast(I32), 0)
-        nc.gpsimd.memset(raw_s[0][:].bitcast(I32), 0)
+        nc.vector.memset(raw_s[0][:].bitcast(I32), 0)
         nc.vector.memset(raw_s[1][:].bitcast(I32), 0)
         nc.vector.memset(raw_s[2][:].bitcast(I32), 0)
 
@@ -74,14 +73,14 @@ def tile_picked_twlgatebegc_none_po_kernel(
         load_scale_rows([nc.scalar, nc.scalar, nc.sync, nc.sync], xs, x_scales)
         nc.sync.dma_start(out=xw[:].bitcast(I32), in_=x_words[0].rearrange("p n t -> p (n t)").bitcast(I32))
         load_scale_rows([nc.sync] * 4, raw_s[1], w2_scales)
-        load_scale_rows([nc.gpsimd] * 4, raw_s[0], w1_scales)
         nc.sync.dma_start(out=raw_w[1][:].bitcast(I32), in_=w2_words[0].bitcast(I32))
         nc.sync.dma_start(out=raw_w[0][:].bitcast(I32), in_=w1_words[0].bitcast(I32))
-        nc.sync.dma_start(n2_t[:], n2)
+        load_scale_rows([nc.gpsimd] * 3 + [nc.sync], raw_s[0], w1_scales)
+        nc.gpsimd.dma_start(out=raw_w[2][:].bitcast(I32), in_=w3_words[0].bitcast(I32))
         nc.sync.dma_start(out=gn_t[:], in_=gn.rearrange("(p t) o -> p (t o)", t=PACK))
-        nc.sync.dma_start(n1_t[:], n1)
-        nc.sync.dma_start(out=raw_w[2][:].bitcast(I32), in_=w3_words[0].bitcast(I32))
+        nc.sync.dma_start(n2_t[:], n2)
         load_scale_rows([nc.sync] * 4, raw_s[2], w3_scales)
+        nc.sync.dma_start(n1_t[:], n1)
         nc.sync.dma_start(n3_t[:], n3)
         nc.sync.dma_start(out=sl_t[:], in_=sl.rearrange("(p t) o -> p (t o)", t=PACK))
         nc.sync.dma_start(out=th_t[:], in_=th.rearrange("(p t) o -> p (t o)", t=PACK))
@@ -129,13 +128,12 @@ def tile_picked_twlgatebegc_none_po_kernel(
             nc.vector.tensor_copy(xy_w[:, c0:c1], xw[:].indirect(offs_t[:, c0 // 16 : c1 // 16]))
         deal_scales(1, nc.gpsimd, "ws1")
         deal_scales(0, nc.gpsimd, "raw_s1")
+        w.append(new("w2", [P, 2 * H], U8, "raw_s0"))
         nc.gpsimd.tensor_copy(
             out=w[2][:].rearrange("p (t m b) -> p t m b", t=PACK, b=2),
             in_=raw_w[2][:].rearrange("p (m t b) -> p t m b", t=PACK, b=2),
         )
         deal_scales(2, nc.gpsimd, "ws2")
-        nc.gpsimd.tensor_tensor(slth[:], sl_t[:], th_t[:], ALU.mult)
-        nc.gpsimd.tensor_scalar(bias[:], slth[:], -1.0, 0.0, ALU.mult, ALU.add)
 
         gy = [new(f"gy{t}", [P, S], F32) for t in range(PACK)]
         gated = new("gated", [P, PACK, S], F32)
@@ -150,7 +148,10 @@ def tile_picked_twlgatebegc_none_po_kernel(
         for t in range(1, PACK):
             y_ps = bank(PACK + t, f"y{t}")
             product(y_ps[:], 0, t, xy_w[:], xy_s[:])
-            nc.scalar.activation(gy[t][:], y_ps[:], ACT.Copy, scale=gn_t[:, t : t + 1])
+            if t == 1:
+                nc.vector.tensor_scalar(gy[t][:], y_ps[:], gn_t[:, t : t + 1], None, ALU.mult)
+            else:
+                nc.scalar.activation(gy[t][:], y_ps[:], ACT.Copy, scale=gn_t[:, t : t + 1])
         for t in range(PACK):
             nc.vector.tensor_tensor(gated[:, t, :], h[t][:].indirect(n2_t[:]), gy[t][:], ALU.mult)
 
@@ -176,11 +177,15 @@ def tile_picked_twlgatebegc_none_po_kernel(
             c0, c1 = Z_CHUNKS[c]
             nc.vector.quantize_mx(out=zw[:, c0:c1].bitcast(FP8X4), scales=zs[:, c0:c1], in_=zb[c][:])
 
-        combine(0)
-        for c in range(1, len(Z_CHUNKS)):
+        last = len(Z_CHUNKS) - 1
+        for c in range(last):
             combine(c)
-            quantise(c - 1)
-        quantise(len(Z_CHUNKS) - 1)
+        for c in range(last):
+            quantise(c)
+        combine(last)
+        quantise(last)
+
+        nc.vector.scalar_tensor_tensor(bias[:], sl_t[:], -1.0, th_t[:], ALU.mult, ALU.mult)
 
         early = bank(0, "h0_early")
         for c0, c1 in Z_CHUNKS[:-1]:

@@ -2,7 +2,7 @@ from contextlib import ExitStack
 
 import concourse.mybir as mybir
 
-K, T, S, N, H, W = 512, 2048, 512, 512, 512, 2048
+T, S, H, W = 2048, 512, 512, 2048
 FLOPS = 3 * 2 * 512 * 512 * 512
 
 F32 = mybir.dt.float32
@@ -19,18 +19,29 @@ AXIS = mybir.AxisListType
 
 P = 128
 PACK = 4
+QUADRANTS = 4
 MEMBERS = 4
+PER_LIST_COLUMN = 16
+LINE = 4
+
+WIDE_WINDOW = 2 * S
 Z_CHUNKS = ((0, 256), (256, 384), (384, 512))
 OUT_CHUNKS = ((0, 128), (128, 256), (256, 384), (384, 448), (448, 512))
-H_WINDOW = 1024
+EARLY_TILES = 2
+VECTOR_Y_TILE = 1
+SG_BUFS = 4
 
 
 def load_scale_rows(queues, tile, scales):
-    for q in range(4):
+    for q in range(QUADRANTS):
         queues[q].dma_start(
             out=tile[32 * q : 32 * q + 4, :].bitcast(I32),
             in_=scales[0, 4 * q : 4 * q + 4, :].bitcast(I32),
         )
+
+
+def entries(list_tile, j0, j1):
+    return list_tile[:, j0 // PER_LIST_COLUMN : j1 // PER_LIST_COLUMN]
 
 
 def tile_picked_twlgatebegc_none_po_kernel(
@@ -40,196 +51,215 @@ def tile_picked_twlgatebegc_none_po_kernel(
     nc = tc.nc
     with ExitStack() as ctx:
         keep = ctx.enter_context(tc.tile_pool(name="keep", bufs=1))
-        ring = ctx.enter_context(tc.tile_pool(name="ring", bufs=4))
+        ring = ctx.enter_context(tc.tile_pool(name="ring", bufs=SG_BUFS))
         psum = ctx.enter_context(tc.psum_pool(name="psum", bufs=1))
 
-        def new(name, shape, dtype, tag=""):
-            return keep.tile(shape, dtype, name=name, align_bytes=64, tag=tag or name)
+        def new(name, shape, dtype, buffer_of=None):
+            return keep.tile(shape, dtype, name=name, align_bytes=64, tag=buffer_of or name)
 
-        offs_t = new("offs_t", [P, S // 16], U16)
-        two_t = new("two_t", [P, S // 16], U16)
-        n1_t = new("n1_t", [P, S // 16], U16)
-        n2_t = new("n2_t", [P, S // 16], U16)
-        n3_t = new("n3_t", [P, W // 16], U16)
-        xw = new("xw", [P, T], U32)
-        xs = new("xs", [P, T], U8)
-        raw_w = [new(f"raw_w{i}", [P, 2 * H], U8) for i in range(3)]
-        raw_s = [new(f"raw_s{i}", [P, H], U8) for i in range(3)]
-        w = [new(f"w{i}", [P, 2 * H], U8) for i in range(2)]
-        ws = {}
+        def bank(b, name):
+            return psum.tile([P, S], F32, name=name, tag=f"bank{b}")
+
+        offs_t = new("offs_t", [P, S // PER_LIST_COLUMN], U16)
+        two_t = new("two_t", [P, S // PER_LIST_COLUMN], U16)
+        n1_t = new("n1_t", [P, S // PER_LIST_COLUMN], U16)
+        n2_t = new("n2_t", [P, S // PER_LIST_COLUMN], U16)
+        n3_t = new("n3_t", [P, W // PER_LIST_COLUMN], U16)
+        x_word_table = new("x_word_table", [P, T], U32)
+        x_scale_table = new("x_scale_table", [P, T], U8)
+        raw_words = {i: new(f"raw_words{i}", [P, 2 * H], U8) for i in (1, 2, 3)}
+        raw_scales = {i: new(f"raw_scales{i}", [P, H], U8) for i in (1, 2, 3)}
+        dealt_words = {i: new(f"dealt_words{i}", [P, 2 * H], U8) for i in (1, 2)}
+        dealt_scales = {}
         gn_t = new("gn_t", [P, PACK], F32)
         sl_t = new("sl_t", [P, PACK], F32)
         th_t = new("th_t", [P, PACK], F32)
         bias = new("bias", [P, PACK], F32)
-        h = [new(f"h{t}", [P, H_WINDOW], F32) for t in range(PACK)]
+        window = [new(f"window{t}", [P, WIDE_WINDOW], F32) for t in range(PACK)]
 
-        nc.gpsimd.memset(xs[:].bitcast(I32), 0)
-        nc.vector.memset(raw_s[0][:].bitcast(I32), 0)
-        nc.vector.memset(raw_s[1][:].bitcast(I32), 0)
-        nc.vector.memset(raw_s[2][:].bitcast(I32), 0)
+        nc.gpsimd.memset(x_scale_table[:].bitcast(I32), 0)
+        for i in (1, 2, 3):
+            nc.vector.memset(raw_scales[i][:].bitcast(I32), 0)
+
+        def load_words(i, words):
+            nc.sync.dma_start(out=raw_words[i][:].bitcast(I32), in_=words[0].bitcast(I32))
+
+        def load_rows(tile, column):
+            nc.sync.dma_start(out=tile[:], in_=column.rearrange("(p t) o -> p (t o)", t=PACK))
 
         nc.sync.dma_start(two_t[:], two)
         nc.sync.dma_start(offs_t[:], offs)
-        load_scale_rows([nc.scalar, nc.scalar, nc.sync, nc.sync], xs, x_scales)
-        nc.sync.dma_start(out=xw[:].bitcast(I32), in_=x_words[0].rearrange("p n t -> p (n t)").bitcast(I32))
-        load_scale_rows([nc.sync] * 4, raw_s[1], w2_scales)
-        nc.sync.dma_start(out=raw_w[1][:].bitcast(I32), in_=w2_words[0].bitcast(I32))
-        nc.sync.dma_start(out=raw_w[0][:].bitcast(I32), in_=w1_words[0].bitcast(I32))
-        load_scale_rows([nc.gpsimd] * 3 + [nc.sync], raw_s[0], w1_scales)
-        nc.gpsimd.dma_start(out=raw_w[2][:].bitcast(I32), in_=w3_words[0].bitcast(I32))
-        nc.sync.dma_start(out=gn_t[:], in_=gn.rearrange("(p t) o -> p (t o)", t=PACK))
+        load_scale_rows([nc.scalar, nc.scalar, nc.sync, nc.sync], x_scale_table, x_scales)
+        nc.sync.dma_start(
+            out=x_word_table[:].bitcast(I32), in_=x_words[0].rearrange("p n t -> p (n t)").bitcast(I32)
+        )
+        load_scale_rows([nc.sync] * QUADRANTS, raw_scales[2], w2_scales)
+        load_words(2, w2_words)
+        load_words(1, w1_words)
+        load_scale_rows([nc.gpsimd, nc.gpsimd, nc.gpsimd, nc.sync], raw_scales[1], w1_scales)
+        load_rows(gn_t, gn)
         nc.sync.dma_start(n2_t[:], n2)
-        load_scale_rows([nc.sync] * 4, raw_s[2], w3_scales)
+        load_words(3, w3_words)
+        load_scale_rows([nc.sync] * QUADRANTS, raw_scales[3], w3_scales)
         nc.sync.dma_start(n1_t[:], n1)
         nc.sync.dma_start(n3_t[:], n3)
-        nc.sync.dma_start(out=sl_t[:], in_=sl.rearrange("(p t) o -> p (t o)", t=PACK))
-        nc.sync.dma_start(out=th_t[:], in_=th.rearrange("(p t) o -> p (t o)", t=PACK))
+        load_rows(sl_t, sl)
+        load_rows(th_t, th)
         for t in range(PACK):
-            nc.vector.memset(h[t][:, S:], 0.0)
+            nc.vector.memset(window[t][:, S:], 0.0)
 
-        def deal_words(i):
+        warm_in = new("warm_in", [P, 1], F32)
+        warm_out = new("warm_out", [P, 1], F32)
+        nc.vector.memset(warm_in[:], 0.0)
+        nc.scalar.activation(warm_out[:], warm_in[:], ACT.Sigmoid)
+
+        def deal_words_on_scalar(i):
             nc.scalar.copy(
-                out=w[i][:].bitcast(U16).rearrange("p (t m) -> p t m", t=PACK),
-                in_=raw_w[i][:].bitcast(U16).rearrange("p (m t) -> p t m", t=PACK),
+                out=dealt_words[i][:].bitcast(U16).rearrange("p (t m) -> p t m", t=PACK),
+                in_=raw_words[i][:].bitcast(U16).rearrange("p (m t) -> p t m", t=PACK),
             )
 
-        def deal_scales(i, engine, tag):
-            ws[i] = new(f"ws{i}", [P, H], U8, tag)
-            engine.tensor_copy(
-                out=ws[i][:].rearrange("p (t m) -> p t m", t=PACK),
-                in_=raw_s[i][:].rearrange("p (m t) -> p t m", t=PACK),
+        def deal_scales(i, buffer_of=None):
+            dealt_scales[i] = new(f"dealt_scales{i}", [P, H], U8, buffer_of)
+            nc.gpsimd.tensor_copy(
+                out=dealt_scales[i][:].rearrange("p (t m) -> p t m", t=PACK),
+                in_=raw_scales[i][:].rearrange("p (m t) -> p t m", t=PACK),
             )
 
-        def product(out, i, t, codes, scales):
+        def product(out, i, t, words, scales):
             nc.tensor.matmul_mx(
                 out=out,
-                lhsT=w[i][:, 2 * P * t : 2 * P * (t + 1)].bitcast(FP4X4),
-                lhsT_scale=ws[i][:, P * t : P * (t + 1)],
-                rhs=codes.bitcast(FP8X4),
+                lhsT=dealt_words[i][:, 2 * P * t : 2 * P * (t + 1)].bitcast(FP4X4),
+                lhsT_scale=dealt_scales[i][:, P * t : P * (t + 1)],
+                rhs=words.bitcast(FP8X4),
                 rhs_scale=scales,
                 start=True,
                 stop=True,
             )
 
-        def bank(b, name):
-            return psum.tile([P, S], F32, name=name, tag=f"bank{b}")
-
-        xd_s = new("xd_s", [P, S], U8)
-        xd_w = new("xd_w", [P, S], U32)
-        xy_s = new("xy_s", [P, S], U8)
-        xy_w = new("xy_w", [P, S], U32)
-        deal_words(1)
-        deal_words(0)
-        nc.vector.tensor_copy(xd_s[:], xs[:].indirect(two_t[:]))
-        nc.vector.tensor_copy(xd_w[:], xw[:].indirect(two_t[:]))
-        nc.vector.tensor_copy(xy_s[:], xs[:].indirect(offs_t[:]))
-        halves = ((0, S // 2), (S // 2, S))
-        for c0, c1 in halves:
-            nc.vector.tensor_copy(xy_w[:, c0:c1], xw[:].indirect(offs_t[:, c0 // 16 : c1 // 16]))
-        deal_scales(1, nc.gpsimd, "ws1")
-        deal_scales(0, nc.gpsimd, "raw_s1")
-        w.append(new("w2", [P, 2 * H], U8, "raw_s0"))
+        xd_scales = new("xd_scales", [P, S], U8)
+        xd_words = new("xd_words", [P, S], U32)
+        xy_scales = new("xy_scales", [P, S], U8)
+        xy_words = new("xy_words", [P, S], U32)
+        deal_words_on_scalar(2)
+        deal_words_on_scalar(1)
+        nc.vector.tensor_copy(xd_scales[:], x_scale_table[:].indirect(two_t[:]))
+        nc.vector.tensor_copy(xd_words[:], x_word_table[:].indirect(two_t[:]))
+        nc.vector.tensor_copy(xy_scales[:], x_scale_table[:].indirect(offs_t[:]))
+        nc.vector.tensor_copy(xy_words[:], x_word_table[:].indirect(offs_t[:]))
+        deal_scales(2)
+        deal_scales(1, "raw_scales2")
+        dealt_words[3] = new("dealt_words3", [P, 2 * H], U8, "raw_scales1")
         nc.gpsimd.tensor_copy(
-            out=w[2][:].rearrange("p (t m b) -> p t m b", t=PACK, b=2),
-            in_=raw_w[2][:].rearrange("p (m t b) -> p t m b", t=PACK, b=2),
+            out=dealt_words[3][:].rearrange("p (t m b) -> p t m b", t=PACK, b=2),
+            in_=raw_words[3][:].rearrange("p (m t b) -> p t m b", t=PACK, b=2),
         )
-        deal_scales(2, nc.gpsimd, "ws2")
+        deal_scales(3)
 
-        gy = [new(f"gy{t}", [P, S], F32) for t in range(PACK)]
+        gain_y = [new(f"gain_y{t}", [P, S], F32) for t in range(PACK)]
         gated = new("gated", [P, PACK, S], F32)
         for t in range(PACK):
             d_ps = bank(t, f"d{t}")
-            product(d_ps[:], 1, t, xd_w[:], xd_s[:])
-            nc.scalar.activation(h[t][:, :S], d_ps[:], ACT.Sigmoid)
-        for b, (c0, c1) in zip((PACK, 0), halves):
-            y_ps = bank(b, f"y0_{c0}")
-            product(y_ps[:, c0:c1], 0, 0, xy_w[:, c0:c1], xy_s[:, c0:c1])
-            nc.vector.tensor_scalar(gy[0][:, c0:c1], y_ps[:, c0:c1], gn_t[:, 0:1], None, ALU.mult)
-        for t in range(1, PACK):
-            y_ps = bank(PACK + t, f"y{t}")
-            product(y_ps[:], 0, t, xy_w[:], xy_s[:])
-            if t == 1:
-                nc.vector.tensor_scalar(gy[t][:], y_ps[:], gn_t[:, t : t + 1], None, ALU.mult)
-            else:
-                nc.scalar.activation(gy[t][:], y_ps[:], ACT.Copy, scale=gn_t[:, t : t + 1])
-        for t in range(PACK):
-            nc.vector.tensor_tensor(gated[:, t, :], h[t][:].indirect(n2_t[:]), gy[t][:], ALU.mult)
+            product(d_ps[:], 2, t, xd_words[:], xd_scales[:])
+            nc.scalar.activation(window[t][:, :S], d_ps[:], ACT.Sigmoid)
+        half = [new(f"half{c}", [P, PACK, c1 - c0], F32) for c, (c0, c1) in enumerate(Z_CHUNKS)]
 
-        zw = new("zw", [P, S], U32)
-        zs = new("zs", [P, S], U8)
-        zb = [new(f"zb{c}", [P, (c1 - c0) * PACK], BF16) for c, (c0, c1) in enumerate(Z_CHUNKS)]
+        def fetch_half(c, t):
+            c0, c1 = Z_CHUNKS[c]
+            nc.scalar.activation(
+                half[c][:, t, :], gain_y[t][:].indirect(entries(n1_t, c0, c1)), ACT.Copy, scale=0.5
+            )
+
+        gate = [new(f"gate{t}", [P, S], F32) for t in range(EARLY_TILES)]
+        for t in range(EARLY_TILES):
+            nc.vector.tensor_copy(gate[t][:], window[t][:].indirect(n2_t[:]))
+        for t in range(PACK):
+            y_ps = bank(PACK + t, f"y{t}")
+            gain = gn_t[:, t : t + 1]
+            product(y_ps[:], 1, t, xy_words[:], xy_scales[:])
+            if t != VECTOR_Y_TILE:
+                nc.scalar.activation(gain_y[t][:], y_ps[:], ACT.Copy, scale=gain)
+            else:
+                nc.vector.tensor_scalar(gain_y[t][:], y_ps[:], gain, None, ALU.mult)
+                fetch_half(0, 0)
+            if t < EARLY_TILES:
+                nc.vector.scalar_tensor_tensor(gated[:, t, :], y_ps[:], gain, gate[t][:], ALU.mult, ALU.mult)
+            else:
+                nc.vector.tensor_tensor(gated[:, t, :], window[t][:].indirect(n2_t[:]), gain_y[t][:], ALU.mult)
+
+        z_words = new("z_words", [P, S], U32)
+        z_scales = new("z_scales", [P, S], U8)
+        z_bf16 = [new(f"z_bf16_{c}", [P, (c1 - c0) * PACK], BF16) for c, (c0, c1) in enumerate(Z_CHUNKS)]
 
         def combine(c):
             c0, c1 = Z_CHUNKS[c]
-            half = new(f"half{c}", [P, PACK, c1 - c0], F32)
             for t in range(PACK):
-                nc.scalar.activation(
-                    half[:, t, :], gy[t][:].indirect(n1_t[:, c0 // 16 : c1 // 16]), ACT.Copy, scale=0.5
-                )
+                if (c, t) != (0, 0):
+                    fetch_half(c, t)
             nc.vector.tensor_tensor(
-                zb[c][:].rearrange("p (c i t) -> p c t i", i=4, t=PACK),
-                gated[:, :, c0:c1].rearrange("p t (c i) -> p c t i", i=4),
-                half[:].rearrange("p t (c i) -> p c t i", i=4),
+                z_bf16[c][:].rearrange("p (j i t) -> p j t i", i=LINE, t=PACK),
+                gated[:, :, c0:c1].rearrange("p t (j i) -> p j t i", i=LINE),
+                half[c][:].rearrange("p t (j i) -> p j t i", i=LINE),
                 ALU.subtract,
             )
 
-        def quantise(c):
+        def quantise_z(c):
             c0, c1 = Z_CHUNKS[c]
-            nc.vector.quantize_mx(out=zw[:, c0:c1].bitcast(FP8X4), scales=zs[:, c0:c1], in_=zb[c][:])
+            nc.vector.quantize_mx(out=z_words[:, c0:c1].bitcast(FP8X4), scales=z_scales[:, c0:c1], in_=z_bf16[c][:])
 
         last = len(Z_CHUNKS) - 1
         for c in range(last):
             combine(c)
         for c in range(last):
-            quantise(c)
+            quantise_z(c)
         combine(last)
-        quantise(last)
+        quantise_z(last)
 
         nc.vector.scalar_tensor_tensor(bias[:], sl_t[:], -1.0, th_t[:], ALU.mult, ALU.mult)
 
         early = bank(0, "h0_early")
-        for c0, c1 in Z_CHUNKS[:-1]:
-            product(early[:, c0:c1], 2, 0, zw[:, c0:c1], zs[:, c0:c1])
-        last0 = Z_CHUNKS[-1][0]
-        nc.scalar.copy(h[0][:, :last0], early[:, :last0])
+        for c0, c1 in Z_CHUNKS[:last]:
+            product(early[:, c0:c1], 3, 0, z_words[:, c0:c1], z_scales[:, c0:c1])
+        last0 = Z_CHUNKS[last][0]
+        nc.scalar.copy(window[0][:, :last0], early[:, :last0])
         late = bank(1, "h0_late")
-        product(late[:, last0:], 2, 0, zw[:, last0:], zs[:, last0:])
-        nc.scalar.copy(h[0][:, last0:S], late[:, last0:])
+        product(late[:, last0:], 3, 0, z_words[:, last0:], z_scales[:, last0:])
+        nc.scalar.copy(window[0][:, last0:S], late[:, last0:])
         for t in range(1, PACK):
-            h_ps = bank(1 + t, f"h{t}_ps")
-            product(h_ps[:], 2, t, zw[:], zs[:])
-            nc.vector.tensor_copy(h[t][:, :S], h_ps[:])
+            h_ps = bank(1 + t, f"h{t}")
+            product(h_ps[:], 3, t, z_words[:], z_scales[:])
+            nc.vector.tensor_copy(window[t][:, :S], h_ps[:])
 
-        out_rows = out_0.rearrange("(p t) c -> p t c", t=PACK)
-        out_words = out_1[0].rearrange("p n t -> p (n t)").bitcast(I32)
-        osc = new("osc", [P, S], U8)
+        out_rows = out_0.rearrange("(p t) j -> p t j", t=PACK)
+        out_words = out_1[0].rearrange("p j t -> p (j t)").bitcast(I32)
+        res_scales = new("res_scales", [P, S], U8)
         for c, (c0, c1) in enumerate(OUT_CHUNKS):
             n = c1 - c0
             res = new(f"res{c}", [P, PACK, n], F32)
-            rb = new(f"rb{c}", [P, n * PACK], BF16)
-            ow = new(f"ow{c}", [P, n], U32)
+            res_bf16 = new(f"res_bf16_{c}", [P, n * PACK], BF16)
+            res_words = new(f"res_words{c}", [P, n], U32)
             for t in range(PACK):
                 sg = ring.tile([P, MEMBERS * n], F32, name="sg")
                 cnt = ring.tile([P, n], F32, name="cnt")
                 nc.scalar.activation(
                     sg[:],
-                    h[t][:].indirect(n3_t[:, MEMBERS * c0 // 16 : MEMBERS * c1 // 16]),
+                    window[t][:].indirect(entries(n3_t, MEMBERS * c0, MEMBERS * c1)),
                     ACT.Sigmoid,
                     bias=bias[:, t : t + 1],
                     scale=sl_t[:, t : t + 1],
                 )
-                nc.vector.tensor_reduce(cnt[:], sg[:].rearrange("p (c m) -> p c m", m=MEMBERS), AXIS.X, ALU.add)
-                nc.vector.scalar_tensor_tensor(res[:, t, :], cnt[:], -1.5, h[t][:, c0:c1], ALU.add, ALU.max)
+                nc.vector.tensor_reduce(cnt[:], sg[:].rearrange("p (j m) -> p j m", m=MEMBERS), AXIS.X, ALU.add)
+                nc.vector.scalar_tensor_tensor(res[:, t, :], cnt[:], -1.5, window[t][:, c0:c1], ALU.add, ALU.max)
             nc.sync.dma_start(out=out_rows[:, :, c0:c1], in_=res[:])
             nc.vector.tensor_copy(
-                rb[:].rearrange("p (c i t) -> p c t i", i=4, t=PACK),
-                res[:].rearrange("p t (c i) -> p c t i", i=4),
+                res_bf16[:].rearrange("p (j i t) -> p j t i", i=LINE, t=PACK),
+                res[:].rearrange("p t (j i) -> p j t i", i=LINE),
             )
-            nc.vector.quantize_mx(out=ow[:].bitcast(FP8X4), scales=osc[:, c0:c1], in_=rb[:])
-            nc.sync.dma_start(out=out_words[:, c0:c1], in_=ow[:].bitcast(I32))
-        for q in range(4):
+            nc.vector.quantize_mx(out=res_words[:].bitcast(FP8X4), scales=res_scales[:, c0:c1], in_=res_bf16[:])
+            nc.sync.dma_start(out=out_words[:, c0:c1], in_=res_words[:].bitcast(I32))
+        for q in range(QUADRANTS):
             queue = nc.scalar if q % 2 == 0 else nc.sync
             queue.dma_start(
                 out=out_2[0, 4 * q : 4 * q + 4, :].bitcast(I32),
-                in_=osc[32 * q : 32 * q + 4, :].bitcast(I32),
+                in_=res_scales[32 * q : 32 * q + 4, :].bitcast(I32),
             )

@@ -108,11 +108,6 @@ def tile_picked_twlgatebegc_none_po_kernel(
         for t in range(PACK):
             nc.vector.memset(window[t][:, S:], 0.0)
 
-        warm_in = new("warm_in", [P, 1], F32)
-        warm_out = new("warm_out", [P, 1], F32)
-        nc.vector.memset(warm_in[:], 0.0)
-        nc.scalar.activation(warm_out[:], warm_in[:], ACT.Sigmoid)
-
         def deal_words_on_scalar(i):
             nc.scalar.copy(
                 out=dealt_words[i][:].bitcast(U16).rearrange("p (t m) -> p t m", t=PACK),

from contextlib import ExitStack

import concourse.mybir as mybir

T, S, H, W = 2048, 512, 512, 2048
FLOPS = 3 * 2 * 512 * 512 * 512

F32 = mybir.dt.float32
BF16 = mybir.dt.bfloat16
I32 = mybir.dt.int32
U32 = mybir.dt.uint32
U16 = mybir.dt.uint16
U8 = mybir.dt.uint8
FP8X4 = mybir.dt.float8_e4m3fn_x4
FP4X4 = mybir.dt.float4_e2m1fn_x4
ACT = mybir.ActivationFunctionType
ALU = mybir.AluOpType
AXIS = mybir.AxisListType

P = 128
PACK = 4
QUADRANTS = 4
MEMBERS = 4
PER_LIST_COLUMN = 16
LINE = 4

WIDE_WINDOW = 2 * S
Z_CHUNKS = ((0, 256), (256, 384), (384, 512))
OUT_CHUNKS = ((0, 128), (128, 256), (256, 384), (384, 448), (448, 512))
EARLY_TILES = 2
VECTOR_Y_TILE = 1
SG_BUFS = 4


def load_scale_rows(queues, tile, scales):
    for q in range(QUADRANTS):
        queues[q].dma_start(
            out=tile[32 * q : 32 * q + 4, :].bitcast(I32),
            in_=scales[0, 4 * q : 4 * q + 4, :].bitcast(I32),
        )


def entries(list_tile, j0, j1):
    return list_tile[:, j0 // PER_LIST_COLUMN : j1 // PER_LIST_COLUMN]


def tile_picked_twlgatebegc_none_po_kernel(
    tc, x_words, x_scales, w1_words, w1_scales, w2_words, w2_scales, gn, w3_words, w3_scales,
    sl, th, offs, two, n1, n2, n3, out_0, out_1, out_2,
):
    nc = tc.nc
    with ExitStack() as ctx:
        keep = ctx.enter_context(tc.tile_pool(name="keep", bufs=1))
        ring = ctx.enter_context(tc.tile_pool(name="ring", bufs=SG_BUFS))
        psum = ctx.enter_context(tc.psum_pool(name="psum", bufs=1))

        def new(name, shape, dtype, buffer_of=None):
            return keep.tile(shape, dtype, name=name, align_bytes=64, tag=buffer_of or name)

        def bank(b, name):
            return psum.tile([P, S], F32, name=name, tag=f"bank{b}")

        offs_t = new("offs_t", [P, S // PER_LIST_COLUMN], U16)
        two_t = new("two_t", [P, S // PER_LIST_COLUMN], U16)
        n1_t = new("n1_t", [P, S // PER_LIST_COLUMN], U16)
        n2_t = new("n2_t", [P, S // PER_LIST_COLUMN], U16)
        n3_t = new("n3_t", [P, W // PER_LIST_COLUMN], U16)
        x_word_table = new("x_word_table", [P, T], U32)
        x_scale_table = new("x_scale_table", [P, T], U8)
        raw_words = {i: new(f"raw_words{i}", [P, 2 * H], U8) for i in (1, 2, 3)}
        raw_scales = {i: new(f"raw_scales{i}", [P, H], U8) for i in (1, 2, 3)}
        dealt_words = {i: new(f"dealt_words{i}", [P, 2 * H], U8) for i in (1, 2)}
        dealt_scales = {}
        gn_t = new("gn_t", [P, PACK], F32)
        sl_t = new("sl_t", [P, PACK], F32)
        th_t = new("th_t", [P, PACK], F32)
        bias = new("bias", [P, PACK], F32)
        window = [new(f"window{t}", [P, WIDE_WINDOW], F32) for t in range(PACK)]

        nc.gpsimd.memset(x_scale_table[:].bitcast(I32), 0)
        for i in (1, 2, 3):
            nc.vector.memset(raw_scales[i][:].bitcast(I32), 0)

        def load_words(i, words):
            nc.sync.dma_start(out=raw_words[i][:].bitcast(I32), in_=words[0].bitcast(I32))

        def load_rows(tile, column):
            nc.sync.dma_start(out=tile[:], in_=column.rearrange("(p t) o -> p (t o)", t=PACK))

        nc.sync.dma_start(two_t[:], two)
        nc.sync.dma_start(offs_t[:], offs)
        load_scale_rows([nc.scalar, nc.scalar, nc.sync, nc.sync], x_scale_table, x_scales)
        nc.sync.dma_start(
            out=x_word_table[:].bitcast(I32), in_=x_words[0].rearrange("p n t -> p (n t)").bitcast(I32)
        )
        load_scale_rows([nc.sync] * QUADRANTS, raw_scales[2], w2_scales)
        load_words(2, w2_words)
        load_words(1, w1_words)
        load_scale_rows([nc.gpsimd, nc.gpsimd, nc.gpsimd, nc.sync], raw_scales[1], w1_scales)
        load_rows(gn_t, gn)
        nc.sync.dma_start(n2_t[:], n2)
        load_words(3, w3_words)
        load_scale_rows([nc.sync] * QUADRANTS, raw_scales[3], w3_scales)
        nc.sync.dma_start(n1_t[:], n1)
        nc.sync.dma_start(n3_t[:], n3)
        load_rows(sl_t, sl)
        load_rows(th_t, th)
        for t in range(PACK):
            nc.vector.memset(window[t][:, S:], 0.0)

        def deal_words_on_scalar(i):
            nc.scalar.copy(
                out=dealt_words[i][:].bitcast(U16).rearrange("p (t m) -> p t m", t=PACK),
                in_=raw_words[i][:].bitcast(U16).rearrange("p (m t) -> p t m", t=PACK),
            )

        def deal_scales(i, buffer_of=None):
            dealt_scales[i] = new(f"dealt_scales{i}", [P, H], U8, buffer_of)
            nc.gpsimd.tensor_copy(
                out=dealt_scales[i][:].rearrange("p (t m) -> p t m", t=PACK),
                in_=raw_scales[i][:].rearrange("p (m t) -> p t m", t=PACK),
            )

        def product(out, i, t, words, scales):
            nc.tensor.matmul_mx(
                out=out,
                lhsT=dealt_words[i][:, 2 * P * t : 2 * P * (t + 1)].bitcast(FP4X4),
                lhsT_scale=dealt_scales[i][:, P * t : P * (t + 1)],
                rhs=words.bitcast(FP8X4),
                rhs_scale=scales,
                start=True,
                stop=True,
            )

        xd_scales = new("xd_scales", [P, S], U8)
        xd_words = new("xd_words", [P, S], U32)
        xy_scales = new("xy_scales", [P, S], U8)
        xy_words = new("xy_words", [P, S], U32)
        deal_words_on_scalar(2)
        deal_words_on_scalar(1)
        nc.vector.tensor_copy(xd_scales[:], x_scale_table[:].indirect(two_t[:]))
        nc.vector.tensor_copy(xd_words[:], x_word_table[:].indirect(two_t[:]))
        nc.vector.tensor_copy(xy_scales[:], x_scale_table[:].indirect(offs_t[:]))
        nc.vector.tensor_copy(xy_words[:], x_word_table[:].indirect(offs_t[:]))
        deal_scales(2)
        deal_scales(1, "raw_scales2")
        dealt_words[3] = new("dealt_words3", [P, 2 * H], U8, "raw_scales1")
        nc.gpsimd.tensor_copy(
            out=dealt_words[3][:].rearrange("p (t m b) -> p t m b", t=PACK, b=2),
            in_=raw_words[3][:].rearrange("p (m t b) -> p t m b", t=PACK, b=2),
        )
        deal_scales(3)

        gain_y = [new(f"gain_y{t}", [P, S], F32) for t in range(PACK)]
        gated = new("gated", [P, PACK, S], F32)
        for t in range(PACK):
            d_ps = bank(t, f"d{t}")
            product(d_ps[:], 2, t, xd_words[:], xd_scales[:])
            nc.scalar.activation(window[t][:, :S], d_ps[:], ACT.Sigmoid)
        half = [new(f"half{c}", [P, PACK, c1 - c0], F32) for c, (c0, c1) in enumerate(Z_CHUNKS)]

        def fetch_half(c, t):
            c0, c1 = Z_CHUNKS[c]
            nc.scalar.activation(
                half[c][:, t, :], gain_y[t][:].indirect(entries(n1_t, c0, c1)), ACT.Copy, scale=0.5
            )

        gate = [new(f"gate{t}", [P, S], F32) for t in range(EARLY_TILES)]
        for t in range(EARLY_TILES):
            nc.vector.tensor_copy(gate[t][:], window[t][:].indirect(n2_t[:]))
        for t in range(PACK):
            y_ps = bank(PACK + t, f"y{t}")
            gain = gn_t[:, t : t + 1]
            product(y_ps[:], 1, t, xy_words[:], xy_scales[:])
            if t != VECTOR_Y_TILE:
                nc.scalar.activation(gain_y[t][:], y_ps[:], ACT.Copy, scale=gain)
            else:
                nc.vector.tensor_scalar(gain_y[t][:], y_ps[:], gain, None, ALU.mult)
                fetch_half(0, 0)
            if t < EARLY_TILES:
                nc.vector.scalar_tensor_tensor(gated[:, t, :], y_ps[:], gain, gate[t][:], ALU.mult, ALU.mult)
            else:
                nc.vector.tensor_tensor(gated[:, t, :], window[t][:].indirect(n2_t[:]), gain_y[t][:], ALU.mult)

        z_words = new("z_words", [P, S], U32)
        z_scales = new("z_scales", [P, S], U8)
        z_bf16 = [new(f"z_bf16_{c}", [P, (c1 - c0) * PACK], BF16) for c, (c0, c1) in enumerate(Z_CHUNKS)]

        def combine(c):
            c0, c1 = Z_CHUNKS[c]
            for t in range(PACK):
                if (c, t) != (0, 0):
                    fetch_half(c, t)
            nc.vector.tensor_tensor(
                z_bf16[c][:].rearrange("p (j i t) -> p j t i", i=LINE, t=PACK),
                gated[:, :, c0:c1].rearrange("p t (j i) -> p j t i", i=LINE),
                half[c][:].rearrange("p t (j i) -> p j t i", i=LINE),
                ALU.subtract,
            )

        def quantise_z(c):
            c0, c1 = Z_CHUNKS[c]
            nc.vector.quantize_mx(out=z_words[:, c0:c1].bitcast(FP8X4), scales=z_scales[:, c0:c1], in_=z_bf16[c][:])

        last = len(Z_CHUNKS) - 1
        for c in range(last):
            combine(c)
        for c in range(last):
            quantise_z(c)
        combine(last)
        quantise_z(last)

        nc.vector.scalar_tensor_tensor(bias[:], sl_t[:], -1.0, th_t[:], ALU.mult, ALU.mult)

        early = bank(0, "h0_early")
        for c0, c1 in Z_CHUNKS[:last]:
            product(early[:, c0:c1], 3, 0, z_words[:, c0:c1], z_scales[:, c0:c1])
        last0 = Z_CHUNKS[last][0]
        nc.scalar.copy(window[0][:, :last0], early[:, :last0])
        late = bank(1, "h0_late")
        product(late[:, last0:], 3, 0, z_words[:, last0:], z_scales[:, last0:])
        nc.scalar.copy(window[0][:, last0:S], late[:, last0:])
        for t in range(1, PACK):
            h_ps = bank(1 + t, f"h{t}")
            product(h_ps[:], 3, t, z_words[:], z_scales[:])
            nc.vector.tensor_copy(window[t][:, :S], h_ps[:])

        out_rows = out_0.rearrange("(p t) j -> p t j", t=PACK)
        out_words = out_1[0].rearrange("p j t -> p (j t)").bitcast(I32)
        res_scales = new("res_scales", [P, S], U8)
        for c, (c0, c1) in enumerate(OUT_CHUNKS):
            n = c1 - c0
            res = new(f"res{c}", [P, PACK, n], F32)
            res_bf16 = new(f"res_bf16_{c}", [P, n * PACK], BF16)
            res_words = new(f"res_words{c}", [P, n], U32)
            for t in range(PACK):
                sg = ring.tile([P, MEMBERS * n], F32, name="sg")
                cnt = ring.tile([P, n], F32, name="cnt")
                nc.scalar.activation(
                    sg[:],
                    window[t][:].indirect(entries(n3_t, MEMBERS * c0, MEMBERS * c1)),
                    ACT.Sigmoid,
                    bias=bias[:, t : t + 1],
                    scale=sl_t[:, t : t + 1],
                )
                nc.vector.tensor_reduce(cnt[:], sg[:].rearrange("p (j m) -> p j m", m=MEMBERS), AXIS.X, ALU.add)
                nc.vector.scalar_tensor_tensor(res[:, t, :], cnt[:], -1.5, window[t][:, c0:c1], ALU.add, ALU.max)
            nc.sync.dma_start(out=out_rows[:, :, c0:c1], in_=res[:])
            nc.vector.tensor_copy(
                res_bf16[:].rearrange("p (j i t) -> p j t i", i=LINE, t=PACK),
                res[:].rearrange("p t (j i) -> p j t i", i=LINE),
            )
            nc.vector.quantize_mx(out=res_words[:].bitcast(FP8X4), scales=res_scales[:, c0:c1], in_=res_bf16[:])
            nc.sync.dma_start(out=out_words[:, c0:c1], in_=res_words[:].bitcast(I32))
        for q in range(QUADRANTS):
            queue = nc.scalar if q % 2 == 0 else nc.sync
            queue.dma_start(
                out=out_2[0, 4 * q : 4 * q + 4, :].bitcast(I32),
                in_=res_scales[32 * q : 32 * q + 4, :].bitcast(I32),
            )
